import numpy as np
import ml_dtypes


def mxq(x, axis, fmt="e4m3"):
    dtype, down = {"e4m3": (ml_dtypes.float8_e4m3fn, 7), "e5m2": (ml_dtypes.float8_e5m2, 14)}[fmt]
    v = np.moveaxis(np.asarray(x, np.float32).astype(ml_dtypes.bfloat16).astype(np.float64), axis, -1)
    blocks = v.reshape(v.shape[:-1] + (-1, 32))
    amax = np.abs(blocks).max(-1, keepdims=True)
    byte = np.maximum(np.where(amax > 0, np.frexp(amax)[1] - 1 + 127, 0) - down, 1)
    scale = np.exp2(byte - 127.0)
    codes = (blocks / scale).astype(np.float32).astype(dtype).astype(np.float64)
    return np.moveaxis((codes * scale).reshape(v.shape), -1, axis)


WIDE = False


def mx_kscale(k):
    if not WIDE:
        return np.ones(k)
    levels = np.array([10, -10, 5, -5, 0])
    if k % 512:
        return np.exp2(np.random.permutation(np.resize(levels, k // 32))).repeat(32)
    a = np.empty((k // 512, 16))
    for p in range(k // 512):
        a[p, :8] = np.random.permutation(np.resize(levels, 8))
        for g in range(8):
            far = levels[np.abs(levels - a[p, g]) >= 10]
            a[p, g + 8] = far[np.random.randint(len(far))]
    return np.exp2(a.ravel()).repeat(32)


def f64(x):
    return np.asarray(x).astype(np.float64)


def striped8(idx):
    return np.asarray(idx).reshape(8, -1, 16).transpose(0, 2, 1).reshape(128, -1).astype(np.uint16)


def unstriped8(offs):
    return offs.reshape(8, 16, -1).transpose(0, 2, 1).reshape(8, -1).astype(np.int64)


def pick8(x, idx, run):
    r = np.arange(len(x))
    return x[r[:, None], idx[r % (8 * run) // run]]


E2M1 = np.array([0.0, 0.5, 1.0, 1.5, 2.0, 3.0, 4.0, 6.0, -0.0, -0.5, -1.0, -1.5, -2.0, -3.0, -4.0, -6.0])


def pack_weight(w, fmt):
    k, n = w.shape
    w = f64(np.asarray(w, np.float32).astype(ml_dtypes.bfloat16)).reshape(k // 32, 32, n)
    amax = np.abs(w).max(1)
    if fmt == "e4m3":
        byte = np.frexp(amax)[1] - 1 + 127 - 7
    else:
        mant, ex = np.frexp(amax / 6.0)
        byte = np.where(mant > 0.5, ex, ex - 1) + 127
    byte = np.clip(np.where(amax > 0, byte, 1), 1, 254)
    scaled = (w * np.exp2(127.0 - byte)[:, None, :]).reshape(k, n).astype(np.float32)
    by_word = np.ascontiguousarray(scaled.reshape(k // 512, 128, 4, n).transpose(0, 1, 3, 2))
    if fmt == "e4m3":
        words = by_word.astype(ml_dtypes.float8_e4m3fn).view(np.uint8)
    else:
        c = by_word.astype(ml_dtypes.float4_e2m1fn).view(np.uint8) & 0xF
        words = (c[..., 0::2] | (c[..., 1::2] << 4)).reshape(k // 512, 128, 2 * n)
    return np.ascontiguousarray(words), np.ascontiguousarray(byte.astype(np.uint8).reshape(k // 512, 16, n))


def unpack_weight(words, scales, fmt):
    g, _, n = scales.shape
    words = np.ascontiguousarray(words).reshape(g, 128, n, -1)
    if fmt == "e4m3":
        vals = words.view(ml_dtypes.float8_e4m3fn).astype(np.float64)
    else:
        nib = np.empty((g, 128, n, 4), np.uint8)
        nib[..., 0::2] = words & 0xF
        nib[..., 1::2] = words >> 4
        vals = E2M1[nib]
    vals = vals * np.repeat(np.exp2(scales.astype(np.float64) - 127.0), 8, axis=1)[..., None]
    return vals.transpose(0, 1, 3, 2).reshape(g * 512, n)


D, K, T, U, I, Q = 512, 512, 1024, 1024, 512, 128


def setup_inputs():
    n = np.random.standard_normal
    idx = np.stack([np.random.permutation(U)[:I] for _ in range(8)])
    idx2 = np.stack([np.random.permutation(U)[:I] for _ in range(8)])
    idx3 = np.stack([np.random.permutation(U)[:I] for _ in range(8)])
    idx4 = np.stack([np.random.permutation(T)[:I] for _ in range(8)])
    idx5 = np.stack([np.random.permutation(U)[:I] for _ in range(8)])
    idx6 = np.stack([np.random.permutation(U)[:I] for _ in range(8)])
    fd = mx_kscale(D)
    fk = mx_kscale(K)
    wqp = pack_weight(n((D, K)) * 1.0 / np.sqrt(D) * fd[:, None] * fk, "e4m3")
    cachep = pack_weight(n((K, T)) * 1.0 / np.sqrt(K) / fk[:, None], "e4m3")
    draftp = pack_weight(n((D, U)) * 1.0 / np.sqrt(D) * fd[:, None], "e2m1")
    return {
        "states": (n((D, Q)) * 0.95 / fd[:, None]).astype(np.float32),
        "wq_words": wqp[0],
        "wq_scales": wqp[1],
        "cache_words": cachep[0],
        "cache_scales": cachep[1],
        "draft_words": draftp[0],
        "draft_scales": draftp[1],
        "offs": striped8(idx),
        "offs2": striped8(idx2),
        "offs3": striped8(idx3),
        "offs4": striped8(idx4),
        "offs5": striped8(idx5),
        "offs6": striped8(idx6),
    }


def reference(states, wq_words, wq_scales, cache_words, cache_scales, draft_words, draft_scales, offs, offs2, offs3, offs4, offs5, offs6):
    idx = unstriped8(offs)
    idx2 = unstriped8(offs2)
    idx3 = unstriped8(offs3)
    idx4 = unstriped8(offs4)
    idx5 = unstriped8(offs5)
    idx6 = unstriped8(offs6)
    wqu = unpack_weight(wq_words, wq_scales, "e4m3")
    cacheu = unpack_weight(cache_words, cache_scales, "e4m3")
    draftu = unpack_weight(draft_words, draft_scales, "e2m1")
    statesq = mxq(f64(states), 0, "e4m3")
    qv = wqu.T @ statesq
    qvq = mxq(qv, 0, "e4m3")
    a = qvq.T @ cacheu
    b = statesq.T @ draftu
    nb = np.zeros((Q, U))
    nb[np.arange(Q)[:, None], idx2[np.arange(Q) % 128 // 16]] = pick8(b, idx, 16)
    n2 = np.zeros((Q, U))
    n2[np.arange(Q)[:, None], idx5[np.arange(Q) % 128 // 16]] = pick8(nb, idx3, 16)
    m1 = np.maximum(n2, b)
    w = pick8(m1, idx6, 16) + pick8(a, idx4, 16)
    y = w - pick8(nb, idx3, 16)
    return y

@@ -1,0 +1,168 @@
+from contextlib import ExitStack
+
+import concourse.mybir as mybir
+from concourse.masks import make_identity
+
+F32 = mybir.dt.float32
+BF16 = mybir.dt.bfloat16
+I32 = mybir.dt.int32
+U32 = mybir.dt.uint32
+U16 = mybir.dt.uint16
+U8 = mybir.dt.uint8
+FP8X4 = mybir.dt.float8_e4m3fn_x4
+FP4X4 = mybir.dt.float4_e2m1fn_x4
+COPY = mybir.ActivationFunctionType.Copy
+ALU = mybir.AluOpType
+
+P = 128
+PACK = 4
+K = 512
+TOKENS = 1024
+SLOTS = 512
+CHUNK = 256
+HALF = SLOTS // 2
+HALF_COLS = HALF // 16
+
+FLOPS = 2 * 512 * P * (K + 2 * TOKENS)
+
+
+def tile_attend_parentpath_side_kernel(tc, states, wq_words, wq_scales, cache_words, cache_scales,
+                                        draft_words, draft_scales, offs, offs2, offs3, offs4, offs5, offs6, out):
+    nc = tc.nc
+    with ExitStack() as ctx:
+        pool = ctx.enter_context(tc.tile_pool(name="pool", bufs=1))
+        psum = ctx.enter_context(tc.psum_pool(name="psum", bufs=1))
+
+        def staged_plane(name, width):
+            plane = pool.tile([P, 4 * width], U8, name=name, align_bytes=64)
+            nc.vector.memset(plane[:, 0:width].bitcast(U32), 0)
+            return plane
+
+        def load_staged(plane, scales):
+            nc.sync.dma_start(out=plane[0:4, :].bitcast(I32).rearrange("r (g c) -> r g c", g=4),
+                              in_=scales[0].bitcast(I32).rearrange("(g r) c -> r g c", g=4))
+
+        def spread_staged(plane, width):
+            for quad in range(1, 4):
+                nc.vector.tensor_copy(out=plane[32 * quad:32 * quad + 4, 0:width].bitcast(I32),
+                                      in_=plane[0:4, quad * width:(quad + 1) * width].bitcast(I32))
+
+        def load_list(name, source):
+            tile = pool.tile([P, SLOTS // 16], U16, name=name)
+            nc.sync.dma_start(tile[:], source)
+            return tile
+
+        def halves(offsets):
+            return [offsets[:, h * HALF_COLS:(h + 1) * HALF_COLS] for h in range(2)]
+
+        slot_half = [slice(h * HALF, (h + 1) * HALF) for h in range(2)]
+
+        draft_plane = pool.tile([P, TOKENS], U8, name="draft_plane", align_bytes=64)
+        nc.gpsimd.memset(draft_plane[:].bitcast(U32), 0)
+        wq_plane = staged_plane("wq_plane", K)
+        cache_plane = pool.tile([P, TOKENS], U8, name="cache_plane", align_bytes=64)
+        nc.vector.memset(cache_plane[:].bitcast(U32), 0)
+        nb = pool.tile([P, TOKENS], F32, name="nb")
+        nc.vector.memset(nb[:], 0.0)
+        n2 = pool.tile([P, TOKENS], F32, name="n2")
+        nc.vector.memset(n2[:], 0.0)
+        identity = pool.tile([P, P], F32, name="identity")
+        make_identity(nc, identity[:])
+
+        states_raw = pool.tile([P, PACK, P], F32, name="states_raw")
+        nc.sync.dma_start(out=states_raw[:], in_=states.rearrange("(p t) q -> p t q", t=PACK))
+        for quad in range(4):
+            nc.sync.dma_start(out=draft_plane[32 * quad:32 * quad + 4, :].bitcast(I32),
+                              in_=draft_scales[0, 4 * quad:4 * quad + 4, :].bitcast(I32))
+        load_staged(wq_plane, wq_scales)
+        draft_codes = pool.tile([P, 2 * TOKENS], U8, name="draft_codes", align_bytes=64)
+        nc.sync.dma_start(out=draft_codes[:].bitcast(I32), in_=draft_words[0].bitcast(I32))
+        wq_codes = pool.tile([P, K], I32, name="wq_codes", align_bytes=64)
+        nc.sync.dma_start(out=wq_codes[:], in_=wq_words[0].rearrange("p n t -> p (n t)").bitcast(I32))
+        idx = load_list("idx", offs)
+        idx2 = load_list("idx2", offs2)
+        cache_codes = pool.tile([P, TOKENS], I32, name="cache_codes", tag="cache_then_picked", align_bytes=64)
+        nc.sync.dma_start(out=cache_codes[:], in_=cache_words[0].rearrange("p n t -> p (n t)").bitcast(I32))
+        for quad in range(4):
+            nc.sync.dma_start(out=cache_plane[32 * quad:32 * quad + 4, :].bitcast(I32),
+                              in_=cache_scales[0, 4 * quad:4 * quad + 4, :].bitcast(I32))
+        idx3 = load_list("idx3", offs3)
+        idx5 = load_list("idx5", offs5)
+        idx4 = load_list("idx4", offs4)
+        idx6 = load_list("idx6", offs6)
+
+        states_bf = pool.tile([P, P, PACK], BF16, name="states_bf", align_bytes=64)
+        nc.vector.tensor_copy(out=states_bf[:], in_=states_raw[:].rearrange("p t q -> p q t"))
+        states_codes = pool.tile([P, P], U32, name="states_codes", align_bytes=64)
+        states_plane = pool.tile([P, P], U8, name="states_plane", align_bytes=64)
+        nc.vector.quantize_mx(out=states_codes[:].bitcast(FP8X4), scales=states_plane[:],
+                              in_=states_bf[:].rearrange("p q t -> p (q t)"))
+
+        spread_staged(wq_plane, K)
+
+        b = pool.tile([P, TOKENS], F32, name="b")
+        edges = [0, 256, 512, 768, 896, 1024]
+        for c in range(5):
+            cols = slice(edges[c], edges[c + 1])
+            bank = psum.tile([P, edges[c + 1] - edges[c]], F32, name="b_bank%d" % c, tag="bank%d" % c)
+            nc.tensor.matmul_mx(out=bank[:], lhsT=states_codes[:].bitcast(FP8X4), lhsT_scale=states_plane[:],
+                                rhs=draft_codes[:, 2 * edges[c]:2 * edges[c + 1]].bitcast(FP4X4),
+                                rhs_scale=draft_plane[:, cols], start=True, stop=True)
+            if c in (0, 2):
+                nc.scalar.activation(b[:, cols], bank[:], COPY)
+            else:
+                nc.vector.tensor_copy(out=b[:, cols], in_=bank[:])
+
+        qv_rows = pool.tile([P, 2, P, 2], BF16, name="qv_rows")
+        for c in range(K // CHUNK):
+            cols = slice(c * CHUNK, (c + 1) * CHUNK)
+            bank = psum.tile([P, CHUNK], F32, name="qv_bank%d" % c)
+            nc.tensor.matmul_mx(out=bank[:], lhsT=states_codes[:].bitcast(FP8X4), lhsT_scale=states_plane[:],
+                                rhs=wq_codes[:, cols].bitcast(FP8X4), rhs_scale=wq_plane[:, cols],
+                                start=True, stop=True)
+            nc.scalar.activation(qv_rows[:, :, 64 * c:64 * (c + 1), :],
+                                 bank[:].rearrange("q (p u e) -> q u p e", u=2, e=2), COPY)
+
+        parents = pool.tile([P, SLOTS], F32, name="parents")
+        for h in range(2):
+            nc.vector.tensor_copy(parents[:, slot_half[h]], b[:].indirect(halves(idx)[h]))
+            nc.scalar.activation(nb[:].indirect(halves(idx2)[h]), parents[:, slot_half[h]], COPY)
+
+        qv_pairs = qv_rows[:].rearrange("q u p e -> q (u p e)").bitcast(F32)
+        turned = psum.tile([P, 2, P], F32, name="turned")
+        for u in range(2):
+            nc.tensor.transpose(turned[:, u, :], qv_pairs[:, u * P:(u + 1) * P], identity[:])
+        qv_bf = pool.tile([P, P * PACK], BF16, name="qv_bf", align_bytes=64)
+        nc.vector.tensor_copy(out=qv_bf[:].bitcast(F32).rearrange("p (q u) -> p q u", u=2),
+                              in_=turned[:].rearrange("p u q -> p q u"))
+        qv_codes = pool.tile([P, P], U32, name="qv_codes", align_bytes=64)
+        qv_plane = pool.tile([P, P], U8, name="qv_plane", align_bytes=64)
+        nc.vector.quantize_mx(out=qv_codes[:].bitcast(FP8X4), scales=qv_plane[:], in_=qv_bf[:])
+
+        a = pool.tile([P, TOKENS], F32, name="a", tag="a_then_m1")
+        for c in range(TOKENS // CHUNK):
+            cols = slice(c * CHUNK, (c + 1) * CHUNK)
+            bank = psum.tile([P, CHUNK], F32, name="a_bank%d" % c, tag="bank%d" % c)
+            nc.tensor.matmul_mx(out=bank[:], lhsT=qv_codes[:].bitcast(FP8X4), lhsT_scale=qv_plane[:],
+                                rhs=cache_codes[:, cols].bitcast(FP8X4),
+                                rhs_scale=cache_plane[:, cols], start=True, stop=True)
+            nc.vector.tensor_copy(out=a[:, cols], in_=bank[:])
+
+        picked = pool.tile([P, SLOTS], F32, name="picked", tag="cache_then_picked", align_bytes=64)
+        for h in range(2):
+            nc.vector.tensor_copy(picked[:, slot_half[h]], nb[:].indirect(halves(idx3)[h]))
+            nc.scalar.activation(n2[:].indirect(halves(idx5)[h]), picked[:, slot_half[h]], COPY)
+
+        side = pool.tile([P, SLOTS], F32, name="side")
+        nc.vector.tensor_tensor(side[:], a[:].indirect(idx4[:]), picked[:], ALU.subtract)
+
+        m1 = pool.tile([P, TOKENS], F32, name="m1", tag="a_then_m1")
+        nc.vector.tensor_tensor(m1[:], n2[:], b[:], ALU.max)
+
+        result = [pool.tile([P, HALF], F32, name="result%d" % h) for h in range(2)]
+        late = pool.tile([P, HALF], F32, name="late")
+        nc.scalar.activation(late[:], m1[:].indirect(halves(idx6)[1]), COPY)
+        nc.vector.tensor_tensor(result[0][:], m1[:].indirect(halves(idx6)[0]), side[:, slot_half[0]], ALU.add)
+        nc.sync.dma_start(out=out[:, slot_half[0]], in_=result[0][:])
+        nc.vector.tensor_tensor(result[1][:], late[:], side[:, slot_half[1]], ALU.add)
+        nc.sync.dma_start(out=out[:, slot_half[1]], in_=result[1][:])

@@ -33,20 +33,6 @@ def tile_attend_parentpath_side_kernel(tc, states, wq_words, wq_scales, cache_wo
         pool = ctx.enter_context(tc.tile_pool(name="pool", bufs=1))
         psum = ctx.enter_context(tc.psum_pool(name="psum", bufs=1))
 
-        def staged_plane(name, width):
-            plane = pool.tile([P, 4 * width], U8, name=name, align_bytes=64)
-            nc.vector.memset(plane[:, 0:width].bitcast(U32), 0)
-            return plane
-
-        def load_staged(plane, scales):
-            nc.sync.dma_start(out=plane[0:4, :].bitcast(I32).rearrange("r (g c) -> r g c", g=4),
-                              in_=scales[0].bitcast(I32).rearrange("(g r) c -> r g c", g=4))
-
-        def spread_staged(plane, width):
-            for quad in range(1, 4):
-                nc.vector.tensor_copy(out=plane[32 * quad:32 * quad + 4, 0:width].bitcast(I32),
-                                      in_=plane[0:4, quad * width:(quad + 1) * width].bitcast(I32))
-
         def load_list(name, source):
             tile = pool.tile([P, SLOTS // 16], U16, name=name)
             nc.sync.dma_start(tile[:], source)
@@ -58,8 +44,9 @@ def tile_attend_parentpath_side_kernel(tc, states, wq_words, wq_scales, cache_wo
         slot_half = [slice(h * HALF, (h + 1) * HALF) for h in range(2)]
 
         draft_plane = pool.tile([P, TOKENS], U8, name="draft_plane", align_bytes=64)
-        nc.gpsimd.memset(draft_plane[:].bitcast(U32), 0)
-        wq_plane = staged_plane("wq_plane", K)
+        nc.vector.memset(draft_plane[:].bitcast(U32), 0)
+        wq_plane = pool.tile([P, K], U8, name="wq_plane", align_bytes=64)
+        nc.vector.memset(wq_plane[:].bitcast(U32), 0)
         cache_plane = pool.tile([P, TOKENS], U8, name="cache_plane", align_bytes=64)
         nc.vector.memset(cache_plane[:].bitcast(U32), 0)
         nb = pool.tile([P, TOKENS], F32, name="nb")
@@ -71,18 +58,24 @@ def tile_attend_parentpath_side_kernel(tc, states, wq_words, wq_scales, cache_wo
 
         states_raw = pool.tile([P, PACK, P], F32, name="states_raw")
         nc.sync.dma_start(out=states_raw[:], in_=states.rearrange("(p t) q -> p t q", t=PACK))
+        draft_codes = pool.tile([P, 2 * TOKENS], U8, name="draft_codes", align_bytes=64)
+        nc.sync.dma_start(out=draft_codes[:].bitcast(I32), in_=draft_words[0].bitcast(I32))
         for quad in range(4):
             nc.sync.dma_start(out=draft_plane[32 * quad:32 * quad + 4, :].bitcast(I32),
                               in_=draft_scales[0, 4 * quad:4 * quad + 4, :].bitcast(I32))
-        load_staged(wq_plane, wq_scales)
-        draft_codes = pool.tile([P, 2 * TOKENS], U8, name="draft_codes", align_bytes=64)
-        nc.sync.dma_start(out=draft_codes[:].bitcast(I32), in_=draft_words[0].bitcast(I32))
-        wq_codes = pool.tile([P, K], I32, name="wq_codes", align_bytes=64)
-        nc.sync.dma_start(out=wq_codes[:], in_=wq_words[0].rearrange("p n t -> p (n t)").bitcast(I32))
         idx = load_list("idx", offs)
+        wq_codes = pool.tile([P, K], I32, name="wq_codes", tag="wq_then_parents", align_bytes=64)
+        nc.sync.dma_start(out=wq_codes[:], in_=wq_words[0].rearrange("p n t -> p (n t)").bitcast(I32))
+        for quad in range(4):
+            nc.sync.dma_start(out=wq_plane[32 * quad:32 * quad + 4, :].bitcast(I32),
+                              in_=wq_scales[0, 4 * quad:4 * quad + 4, :].bitcast(I32))
         idx2 = load_list("idx2", offs2)
-        cache_codes = pool.tile([P, TOKENS], I32, name="cache_codes", tag="cache_then_picked", align_bytes=64)
-        nc.sync.dma_start(out=cache_codes[:], in_=cache_words[0].rearrange("p n t -> p (n t)").bitcast(I32))
+        cache_all = cache_words[0].rearrange("p n t -> p (n t)").bitcast(I32)
+        cache_codes = []
+        for h, tag in enumerate(("cache_then_picked", "cache_high")):
+            codes = pool.tile([P, 512], I32, name="cache_codes%d" % h, tag=tag, align_bytes=64)
+            nc.sync.dma_start(out=codes[:], in_=cache_all[:, 512 * h:512 * (h + 1)])
+            cache_codes.append(codes)
         for quad in range(4):
             nc.sync.dma_start(out=cache_plane[32 * quad:32 * quad + 4, :].bitcast(I32),
                               in_=cache_scales[0, 4 * quad:4 * quad + 4, :].bitcast(I32))
@@ -92,13 +85,14 @@ def tile_attend_parentpath_side_kernel(tc, states, wq_words, wq_scales, cache_wo
         idx6 = load_list("idx6", offs6)
 
         states_bf = pool.tile([P, P, PACK], BF16, name="states_bf", align_bytes=64)
-        nc.vector.tensor_copy(out=states_bf[:], in_=states_raw[:].rearrange("p t q -> p q t"))
+        by_column = states_raw[:].rearrange("p t q -> p q t")
+        nc.vector.tensor_copy(out=states_bf[:, 0:64, :], in_=by_column[:, 0:64, :])
+        nc.scalar.activation(states_bf[:, 64:P, :], by_column[:, 64:P, :], COPY)
         states_codes = pool.tile([P, P], U32, name="states_codes", align_bytes=64)
         states_plane = pool.tile([P, P], U8, name="states_plane", align_bytes=64)
         nc.vector.quantize_mx(out=states_codes[:].bitcast(FP8X4), scales=states_plane[:],
                               in_=states_bf[:].rearrange("p q t -> p (q t)"))
 
-        spread_staged(wq_plane, K)
 
         b = pool.tile([P, TOKENS], F32, name="b")
         edges = [0, 256, 512, 768, 896, 1024]
@@ -108,25 +102,23 @@ def tile_attend_parentpath_side_kernel(tc, states, wq_words, wq_scales, cache_wo
             nc.tensor.matmul_mx(out=bank[:], lhsT=states_codes[:].bitcast(FP8X4), lhsT_scale=states_plane[:],
                                 rhs=draft_codes[:, 2 * edges[c]:2 * edges[c + 1]].bitcast(FP4X4),
                                 rhs_scale=draft_plane[:, cols], start=True, stop=True)
-            if c in (0, 2):
+            if c not in (0, 2):
                 nc.scalar.activation(b[:, cols], bank[:], COPY)
             else:
                 nc.vector.tensor_copy(out=b[:, cols], in_=bank[:])
 
         qv_rows = pool.tile([P, 2, P, 2], BF16, name="qv_rows")
-        for c in range(K // CHUNK):
-            cols = slice(c * CHUNK, (c + 1) * CHUNK)
-            bank = psum.tile([P, CHUNK], F32, name="qv_bank%d" % c)
-            nc.tensor.matmul_mx(out=bank[:], lhsT=states_codes[:].bitcast(FP8X4), lhsT_scale=states_plane[:],
-                                rhs=wq_codes[:, cols].bitcast(FP8X4), rhs_scale=wq_plane[:, cols],
-                                start=True, stop=True)
-            nc.scalar.activation(qv_rows[:, :, 64 * c:64 * (c + 1), :],
-                                 bank[:].rearrange("q (p u e) -> q u p e", u=2, e=2), COPY)
+        qv_bank = psum.tile([P, K], F32, name="qv_bank", tag="bank4")
+        nc.tensor.matmul_mx(out=qv_bank[:], lhsT=states_codes[:].bitcast(FP8X4), lhsT_scale=states_plane[:],
+                            rhs=wq_codes[:].bitcast(FP8X4), rhs_scale=wq_plane[:], start=True, stop=True)
 
-        parents = pool.tile([P, SLOTS], F32, name="parents")
-        for h in range(2):
-            nc.vector.tensor_copy(parents[:, slot_half[h]], b[:].indirect(halves(idx)[h]))
-            nc.scalar.activation(nb[:].indirect(halves(idx2)[h]), parents[:, slot_half[h]], COPY)
+        parents0 = pool.tile([P, HALF], F32, name="parents0")
+        nc.vector.tensor_copy(parents0[:], b[:].indirect(halves(idx)[0]))
+        nc.scalar.activation(nb[:].indirect(halves(idx2)[0]), parents0[:], COPY)
+        nc.vector.tensor_copy(out=qv_rows[:], in_=qv_bank[:].rearrange("q (p u e) -> q u p e", u=2, e=2))
+        parents1 = pool.tile([P, HALF], F32, name="parents1", tag="wq_then_parents", align_bytes=64)
+        nc.vector.tensor_copy(parents1[:], b[:].indirect(halves(idx)[1]))
+        nc.scalar.activation(nb[:].indirect(halves(idx2)[1]), parents1[:], COPY)
 
         qv_pairs = qv_rows[:].rearrange("q u p e -> q (u p e)").bitcast(F32)
         turned = psum.tile([P, 2, P], F32, name="turned")
@@ -140,19 +132,24 @@ def tile_attend_parentpath_side_kernel(tc, states, wq_words, wq_scales, cache_wo
         nc.vector.quantize_mx(out=qv_codes[:].bitcast(FP8X4), scales=qv_plane[:], in_=qv_bf[:])
 
         a = pool.tile([P, TOKENS], F32, name="a", tag="a_then_m1")
+        a_banks = []
         for c in range(TOKENS // CHUNK):
             cols = slice(c * CHUNK, (c + 1) * CHUNK)
             bank = psum.tile([P, CHUNK], F32, name="a_bank%d" % c, tag="bank%d" % c)
             nc.tensor.matmul_mx(out=bank[:], lhsT=qv_codes[:].bitcast(FP8X4), lhsT_scale=qv_plane[:],
-                                rhs=cache_codes[:, cols].bitcast(FP8X4),
+                                rhs=cache_codes[c // 2][:, (c % 2) * CHUNK:(c % 2 + 1) * CHUNK].bitcast(FP8X4),
                                 rhs_scale=cache_plane[:, cols], start=True, stop=True)
-            nc.vector.tensor_copy(out=a[:, cols], in_=bank[:])
+            a_banks.append(bank)
+            if c < 2:
+                nc.vector.tensor_copy(out=a[:, cols], in_=bank[:])
 
         picked = pool.tile([P, SLOTS], F32, name="picked", tag="cache_then_picked", align_bytes=64)
         for h in range(2):
             nc.vector.tensor_copy(picked[:, slot_half[h]], nb[:].indirect(halves(idx3)[h]))
             nc.scalar.activation(n2[:].indirect(halves(idx5)[h]), picked[:, slot_half[h]], COPY)
 
+        for c in range(2, 4):
+            nc.vector.tensor_copy(out=a[:, c * CHUNK:(c + 1) * CHUNK], in_=a_banks[c][:])
         side = pool.tile([P, SLOTS], F32, name="side")
         nc.vector.tensor_tensor(side[:], a[:].indirect(idx4[:]), picked[:], ALU.subtract)
 

@@ -51,18 +51,17 @@ def tile_attend_parentpath_side_kernel(tc, states, wq_words, wq_scales, cache_wo
         nc.vector.memset(cache_plane[:].bitcast(U32), 0)
         nb = pool.tile([P, TOKENS], F32, name="nb")
         nc.vector.memset(nb[:], 0.0)
-        n2 = pool.tile([P, TOKENS], F32, name="n2")
-        nc.vector.memset(n2[:], 0.0)
         identity = pool.tile([P, P], F32, name="identity")
         make_identity(nc, identity[:])
 
         states_raw = pool.tile([P, PACK, P], F32, name="states_raw")
         nc.sync.dma_start(out=states_raw[:], in_=states.rearrange("(p t) q -> p t q", t=PACK))
-        draft_codes = pool.tile([P, 2 * TOKENS], U8, name="draft_codes", align_bytes=64)
-        nc.sync.dma_start(out=draft_codes[:].bitcast(I32), in_=draft_words[0].bitcast(I32))
+        draft_codes = [pool.tile([P, TOKENS], U8, name="draft_codes%d" % h, align_bytes=64) for h in range(2)]
+        nc.sync.dma_start(out=draft_codes[0][:].bitcast(I32), in_=draft_words[0, :, 0:TOKENS].bitcast(I32))
         for quad in range(4):
             nc.sync.dma_start(out=draft_plane[32 * quad:32 * quad + 4, :].bitcast(I32),
                               in_=draft_scales[0, 4 * quad:4 * quad + 4, :].bitcast(I32))
+        nc.sync.dma_start(out=draft_codes[1][:].bitcast(I32), in_=draft_words[0, :, TOKENS:2 * TOKENS].bitcast(I32))
         idx = load_list("idx", offs)
         wq_codes = pool.tile([P, K], I32, name="wq_codes", tag="wq_then_parents", align_bytes=64)
         nc.sync.dma_start(out=wq_codes[:], in_=wq_words[0].rearrange("p n t -> p (n t)").bitcast(I32))
@@ -84,7 +83,7 @@ def tile_attend_parentpath_side_kernel(tc, states, wq_words, wq_scales, cache_wo
         idx4 = load_list("idx4", offs4)
         idx6 = load_list("idx6", offs6)
 
-        states_bf = pool.tile([P, P, PACK], BF16, name="states_bf", align_bytes=64)
+        states_bf = pool.tile([P, P, PACK], BF16, name="states_bf", tag="states_then_n2", align_bytes=64)
         by_column = states_raw[:].rearrange("p t q -> p q t")
         nc.vector.tensor_copy(out=states_bf[:, 0:64, :], in_=by_column[:, 0:64, :])
         nc.scalar.activation(states_bf[:, 64:P, :], by_column[:, 64:P, :], COPY)
@@ -94,13 +93,16 @@ def tile_attend_parentpath_side_kernel(tc, states, wq_words, wq_scales, cache_wo
                               in_=states_bf[:].rearrange("p q t -> p (q t)"))
 
 
+        n2 = pool.tile([P, TOKENS], F32, name="n2", tag="states_then_n2", align_bytes=64)
+        nc.vector.memset(n2[:], 0.0)
+
         b = pool.tile([P, TOKENS], F32, name="b")
         edges = [0, 256, 512, 768, 896, 1024]
         for c in range(5):
             cols = slice(edges[c], edges[c + 1])
             bank = psum.tile([P, edges[c + 1] - edges[c]], F32, name="b_bank%d" % c, tag="bank%d" % c)
             nc.tensor.matmul_mx(out=bank[:], lhsT=states_codes[:].bitcast(FP8X4), lhsT_scale=states_plane[:],
-                                rhs=draft_codes[:, 2 * edges[c]:2 * edges[c + 1]].bitcast(FP4X4),
+                                rhs=draft_codes[edges[c] // 512][:, 2 * (edges[c] % 512):2 * (edges[c] % 512 + edges[c + 1] - edges[c])].bitcast(FP4X4),
                                 rhs_scale=draft_plane[:, cols], start=True, stop=True)
             if c not in (0, 2):
                 nc.scalar.activation(b[:, cols], bank[:], COPY)

@@ -63,7 +63,7 @@ def tile_attend_parentpath_side_kernel(tc, states, wq_words, wq_scales, cache_wo
                               in_=draft_scales[0, 4 * quad:4 * quad + 4, :].bitcast(I32))
         nc.sync.dma_start(out=draft_codes[1][:].bitcast(I32), in_=draft_words[0, :, TOKENS:2 * TOKENS].bitcast(I32))
         idx = load_list("idx", offs)
-        wq_codes = pool.tile([P, K], I32, name="wq_codes", tag="wq_then_parents", align_bytes=64)
+        wq_codes = pool.tile([P, K], I32, name="wq_codes", align_bytes=64)
         nc.sync.dma_start(out=wq_codes[:], in_=wq_words[0].rearrange("p n t -> p (n t)").bitcast(I32))
         for quad in range(4):
             nc.sync.dma_start(out=wq_plane[32 * quad:32 * quad + 4, :].bitcast(I32),
@@ -104,7 +104,7 @@ def tile_attend_parentpath_side_kernel(tc, states, wq_words, wq_scales, cache_wo
             nc.tensor.matmul_mx(out=bank[:], lhsT=states_codes[:].bitcast(FP8X4), lhsT_scale=states_plane[:],
                                 rhs=draft_codes[edges[c] // 512][:, 2 * (edges[c] % 512):2 * (edges[c] % 512 + edges[c + 1] - edges[c])].bitcast(FP4X4),
                                 rhs_scale=draft_plane[:, cols], start=True, stop=True)
-            if c not in (0, 2):
+            if c in (0, 2):
                 nc.scalar.activation(b[:, cols], bank[:], COPY)
             else:
                 nc.vector.tensor_copy(out=b[:, cols], in_=bank[:])
@@ -114,13 +114,11 @@ def tile_attend_parentpath_side_kernel(tc, states, wq_words, wq_scales, cache_wo
         nc.tensor.matmul_mx(out=qv_bank[:], lhsT=states_codes[:].bitcast(FP8X4), lhsT_scale=states_plane[:],
                             rhs=wq_codes[:].bitcast(FP8X4), rhs_scale=wq_plane[:], start=True, stop=True)
 
-        parents0 = pool.tile([P, HALF], F32, name="parents0")
-        nc.vector.tensor_copy(parents0[:], b[:].indirect(halves(idx)[0]))
-        nc.scalar.activation(nb[:].indirect(halves(idx2)[0]), parents0[:], COPY)
+        parents = pool.tile([P, SLOTS], F32, name="parents")
+        nc.vector.tensor_copy(parents[:, slot_half[0]], b[:].indirect(halves(idx)[0]))
+        nc.scalar.activation(parents[:, slot_half[1]], b[:].indirect(halves(idx)[1]), COPY)
+        nc.scalar.activation(nb[:].indirect(idx2[:]), parents[:], COPY)
         nc.vector.tensor_copy(out=qv_rows[:], in_=qv_bank[:].rearrange("q (p u e) -> q u p e", u=2, e=2))
-        parents1 = pool.tile([P, HALF], F32, name="parents1", tag="wq_then_parents", align_bytes=64)
-        nc.vector.tensor_copy(parents1[:], b[:].indirect(halves(idx)[1]))
-        nc.scalar.activation(nb[:].indirect(halves(idx2)[1]), parents1[:], COPY)
 
         qv_pairs = qv_rows[:].rearrange("q u p e -> q (u p e)").bitcast(F32)
         turned = psum.tile([P, 2, P], F32, name="turned")
@@ -142,15 +140,15 @@ def tile_attend_parentpath_side_kernel(tc, states, wq_words, wq_scales, cache_wo
                                 rhs=cache_codes[c // 2][:, (c % 2) * CHUNK:(c % 2 + 1) * CHUNK].bitcast(FP8X4),
                                 rhs_scale=cache_plane[:, cols], start=True, stop=True)
             a_banks.append(bank)
-            if c < 2:
+            if c < 1:
                 nc.vector.tensor_copy(out=a[:, cols], in_=bank[:])
 
         picked = pool.tile([P, SLOTS], F32, name="picked", tag="cache_then_picked", align_bytes=64)
-        for h in range(2):
-            nc.vector.tensor_copy(picked[:, slot_half[h]], nb[:].indirect(halves(idx3)[h]))
-            nc.scalar.activation(n2[:].indirect(halves(idx5)[h]), picked[:, slot_half[h]], COPY)
+        nc.vector.tensor_copy(picked[:, slot_half[0]], nb[:].indirect(halves(idx3)[0]))
+        nc.scalar.activation(picked[:, slot_half[1]], nb[:].indirect(halves(idx3)[1]), COPY)
+        nc.scalar.activation(n2[:].indirect(idx5[:]), picked[:], COPY)
 
-        for c in range(2, 4):
+        for c in range(1, 4):
             nc.vector.tensor_copy(out=a[:, c * CHUNK:(c + 1) * CHUNK], in_=a_banks[c][:])
         side = pool.tile([P, SLOTS], F32, name="side")
         nc.vector.tensor_tensor(side[:], a[:].indirect(idx4[:]), picked[:], ALU.subtract)

from contextlib import ExitStack

import concourse.mybir as mybir
from concourse.masks import make_identity

F32 = mybir.dt.float32
BF16 = mybir.dt.bfloat16
I32 = mybir.dt.int32
U32 = mybir.dt.uint32
U16 = mybir.dt.uint16
U8 = mybir.dt.uint8
FP8X4 = mybir.dt.float8_e4m3fn_x4
FP4X4 = mybir.dt.float4_e2m1fn_x4
COPY = mybir.ActivationFunctionType.Copy
ALU = mybir.AluOpType

P = 128
PACK = 4
K = 512
TOKENS = 1024
SLOTS = 512
CHUNK = 256
HALF = SLOTS // 2
HALF_COLS = HALF // 16

FLOPS = 2 * 512 * P * (K + 2 * TOKENS)


def tile_attend_parentpath_side_kernel(tc, states, wq_words, wq_scales, cache_words, cache_scales,
                                        draft_words, draft_scales, offs, offs2, offs3, offs4, offs5, offs6, out):
    nc = tc.nc
    with ExitStack() as ctx:
        pool = ctx.enter_context(tc.tile_pool(name="pool", bufs=1))
        psum = ctx.enter_context(tc.psum_pool(name="psum", bufs=1))

        def load_list(name, source):
            tile = pool.tile([P, SLOTS // 16], U16, name=name)
            nc.sync.dma_start(tile[:], source)
            return tile

        def halves(offsets):
            return [offsets[:, h * HALF_COLS:(h + 1) * HALF_COLS] for h in range(2)]

        slot_half = [slice(h * HALF, (h + 1) * HALF) for h in range(2)]

        draft_plane = pool.tile([P, TOKENS], U8, name="draft_plane", align_bytes=64)
        nc.vector.memset(draft_plane[:].bitcast(U32), 0)
        wq_plane = pool.tile([P, K], U8, name="wq_plane", align_bytes=64)
        nc.vector.memset(wq_plane[:].bitcast(U32), 0)
        cache_plane = pool.tile([P, TOKENS], U8, name="cache_plane", align_bytes=64)
        nc.vector.memset(cache_plane[:].bitcast(U32), 0)
        nb = pool.tile([P, TOKENS], F32, name="nb")
        nc.vector.memset(nb[:], 0.0)
        identity = pool.tile([P, P], F32, name="identity")
        make_identity(nc, identity[:])

        states_raw = pool.tile([P, PACK, P], F32, name="states_raw")
        nc.sync.dma_start(out=states_raw[:], in_=states.rearrange("(p t) q -> p t q", t=PACK))
        draft_codes = [pool.tile([P, TOKENS], U8, name="draft_codes%d" % h, align_bytes=64) for h in range(2)]
        nc.sync.dma_start(out=draft_codes[0][:].bitcast(I32), in_=draft_words[0, :, 0:TOKENS].bitcast(I32))
        for quad in range(4):
            nc.sync.dma_start(out=draft_plane[32 * quad:32 * quad + 4, :].bitcast(I32),
                              in_=draft_scales[0, 4 * quad:4 * quad + 4, :].bitcast(I32))
        nc.sync.dma_start(out=draft_codes[1][:].bitcast(I32), in_=draft_words[0, :, TOKENS:2 * TOKENS].bitcast(I32))
        idx = load_list("idx", offs)
        wq_codes = pool.tile([P, K], I32, name="wq_codes", align_bytes=64)
        nc.sync.dma_start(out=wq_codes[:], in_=wq_words[0].rearrange("p n t -> p (n t)").bitcast(I32))
        for quad in range(4):
            nc.sync.dma_start(out=wq_plane[32 * quad:32 * quad + 4, :].bitcast(I32),
                              in_=wq_scales[0, 4 * quad:4 * quad + 4, :].bitcast(I32))
        idx2 = load_list("idx2", offs2)
        cache_all = cache_words[0].rearrange("p n t -> p (n t)").bitcast(I32)
        cache_codes = []
        for h, tag in enumerate(("cache_then_picked", "cache_high")):
            codes = pool.tile([P, 512], I32, name="cache_codes%d" % h, tag=tag, align_bytes=64)
            nc.sync.dma_start(out=codes[:], in_=cache_all[:, 512 * h:512 * (h + 1)])
            cache_codes.append(codes)
        for quad in range(4):
            nc.sync.dma_start(out=cache_plane[32 * quad:32 * quad + 4, :].bitcast(I32),
                              in_=cache_scales[0, 4 * quad:4 * quad + 4, :].bitcast(I32))
        idx3 = load_list("idx3", offs3)
        idx5 = load_list("idx5", offs5)
        idx4 = load_list("idx4", offs4)
        idx6 = load_list("idx6", offs6)

        states_bf = pool.tile([P, P, PACK], BF16, name="states_bf", tag="states_then_n2", align_bytes=64)
        by_column = states_raw[:].rearrange("p t q -> p q t")
        nc.vector.tensor_copy(out=states_bf[:, 0:64, :], in_=by_column[:, 0:64, :])
        nc.scalar.activation(states_bf[:, 64:P, :], by_column[:, 64:P, :], COPY)
        states_codes = pool.tile([P, P], U32, name="states_codes", align_bytes=64)
        states_plane = pool.tile([P, P], U8, name="states_plane", align_bytes=64)
        nc.vector.quantize_mx(out=states_codes[:].bitcast(FP8X4), scales=states_plane[:],
                              in_=states_bf[:].rearrange("p q t -> p (q t)"))


        n2 = pool.tile([P, TOKENS], F32, name="n2", tag="states_then_n2", align_bytes=64)
        nc.vector.memset(n2[:], 0.0)

        b = pool.tile([P, TOKENS], F32, name="b")
        edges = [0, 256, 512, 768, 896, 1024]
        for c in range(5):
            cols = slice(edges[c], edges[c + 1])
            bank = psum.tile([P, edges[c + 1] - edges[c]], F32, name="b_bank%d" % c, tag="bank%d" % c)
            nc.tensor.matmul_mx(out=bank[:], lhsT=states_codes[:].bitcast(FP8X4), lhsT_scale=states_plane[:],
                                rhs=draft_codes[edges[c] // 512][:, 2 * (edges[c] % 512):2 * (edges[c] % 512 + edges[c + 1] - edges[c])].bitcast(FP4X4),
                                rhs_scale=draft_plane[:, cols], start=True, stop=True)
            if c in (0, 2):
                nc.scalar.activation(b[:, cols], bank[:], COPY)
            else:
                nc.vector.tensor_copy(out=b[:, cols], in_=bank[:])

        qv_rows = pool.tile([P, 2, P, 2], BF16, name="qv_rows")
        qv_bank = psum.tile([P, K], F32, name="qv_bank", tag="bank4")
        nc.tensor.matmul_mx(out=qv_bank[:], lhsT=states_codes[:].bitcast(FP8X4), lhsT_scale=states_plane[:],
                            rhs=wq_codes[:].bitcast(FP8X4), rhs_scale=wq_plane[:], start=True, stop=True)

        parents = pool.tile([P, SLOTS], F32, name="parents")
        nc.vector.tensor_copy(parents[:, slot_half[0]], b[:].indirect(halves(idx)[0]))
        nc.scalar.activation(parents[:, slot_half[1]], b[:].indirect(halves(idx)[1]), COPY)
        nc.scalar.activation(nb[:].indirect(idx2[:]), parents[:], COPY)
        nc.vector.tensor_copy(out=qv_rows[:], in_=qv_bank[:].rearrange("q (p u e) -> q u p e", u=2, e=2))

        qv_pairs = qv_rows[:].rearrange("q u p e -> q (u p e)").bitcast(F32)
        turned = psum.tile([P, 2, P], F32, name="turned")
        for u in range(2):
            nc.tensor.transpose(turned[:, u, :], qv_pairs[:, u * P:(u + 1) * P], identity[:])
        qv_bf = pool.tile([P, P * PACK], BF16, name="qv_bf", align_bytes=64)
        nc.vector.tensor_copy(out=qv_bf[:].bitcast(F32).rearrange("p (q u) -> p q u", u=2),
                              in_=turned[:].rearrange("p u q -> p q u"))
        qv_codes = pool.tile([P, P], U32, name="qv_codes", align_bytes=64)
        qv_plane = pool.tile([P, P], U8, name="qv_plane", align_bytes=64)
        nc.vector.quantize_mx(out=qv_codes[:].bitcast(FP8X4), scales=qv_plane[:], in_=qv_bf[:])

        a = pool.tile([P, TOKENS], F32, name="a", tag="a_then_m1")
        a_banks = []
        for c in range(TOKENS // CHUNK):
            cols = slice(c * CHUNK, (c + 1) * CHUNK)
            bank = psum.tile([P, CHUNK], F32, name="a_bank%d" % c, tag="bank%d" % c)
            nc.tensor.matmul_mx(out=bank[:], lhsT=qv_codes[:].bitcast(FP8X4), lhsT_scale=qv_plane[:],
                                rhs=cache_codes[c // 2][:, (c % 2) * CHUNK:(c % 2 + 1) * CHUNK].bitcast(FP8X4),
                                rhs_scale=cache_plane[:, cols], start=True, stop=True)
            a_banks.append(bank)
            if c < 1:
                nc.vector.tensor_copy(out=a[:, cols], in_=bank[:])

        picked = pool.tile([P, SLOTS], F32, name="picked", tag="cache_then_picked", align_bytes=64)
        nc.vector.tensor_copy(picked[:, slot_half[0]], nb[:].indirect(halves(idx3)[0]))
        nc.scalar.activation(picked[:, slot_half[1]], nb[:].indirect(halves(idx3)[1]), COPY)
        nc.scalar.activation(n2[:].indirect(idx5[:]), picked[:], COPY)

        for c in range(1, 4):
            nc.vector.tensor_copy(out=a[:, c * CHUNK:(c + 1) * CHUNK], in_=a_banks[c][:])
        side = pool.tile([P, SLOTS], F32, name="side")
        nc.vector.tensor_tensor(side[:], a[:].indirect(idx4[:]), picked[:], ALU.subtract)

        m1 = pool.tile([P, TOKENS], F32, name="m1", tag="a_then_m1")
        nc.vector.tensor_tensor(m1[:], n2[:], b[:], ALU.max)

        result = [pool.tile([P, HALF], F32, name="result%d" % h) for h in range(2)]
        late = pool.tile([P, HALF], F32, name="late")
        nc.scalar.activation(late[:], m1[:].indirect(halves(idx6)[1]), COPY)
        nc.vector.tensor_tensor(result[0][:], m1[:].indirect(halves(idx6)[0]), side[:, slot_half[0]], ALU.add)
        nc.sync.dma_start(out=out[:, slot_half[0]], in_=result[0][:])
        nc.vector.tensor_tensor(result[1][:], late[:], side[:, slot_half[1]], ALU.add)
        nc.sync.dma_start(out=out[:, slot_half[1]], in_=result[1][:])
